import numpy as np
import ml_dtypes


def mxq(x, axis, fmt="e4m3"):
    dtype, down = {"e4m3": (ml_dtypes.float8_e4m3fn, 7), "e5m2": (ml_dtypes.float8_e5m2, 14)}[fmt]
    v = np.moveaxis(np.asarray(x, np.float32).astype(ml_dtypes.bfloat16).astype(np.float64), axis, -1)
    blocks = v.reshape(v.shape[:-1] + (-1, 32))
    amax = np.abs(blocks).max(-1, keepdims=True)
    byte = np.maximum(np.where(amax > 0, np.frexp(amax)[1] - 1 + 127, 0) - down, 1)
    scale = np.exp2(byte - 127.0)
    codes = (blocks / scale).astype(np.float32).astype(dtype).astype(np.float64)
    return np.moveaxis((codes * scale).reshape(v.shape), -1, axis)


WIDE = False


def mx_kscale(k, group=512):
    if not WIDE:
        return np.ones(k)
    levels = np.array([18, -18])
    if group != 512:
        return np.exp2(np.random.permutation(np.resize(levels, k // group))).repeat(group)
    if k % 512:
        return np.exp2(np.random.permutation(np.resize(levels, k // 32))).repeat(32)
    a = np.empty((k // 512, 16))
    for p in range(k // 512):
        a[p, :8] = np.random.permutation(np.resize(levels, 8))
        for g in range(8):
            far = levels[np.abs(levels - a[p, g]) >= 10]
            a[p, g + 8] = far[np.random.randint(len(far))]
    return np.exp2(a.ravel()).repeat(32)


def f64(x):
    return np.asarray(x).astype(np.float64)


G, D, I, N, J = 4, 128, 128, 512, 128


def sgn(shape):
    return np.random.uniform(0.5, 2.0, shape) * np.where(np.random.standard_normal(shape) < 0, -1.0, 1.0)


def setup_inputs():
    n = np.random.standard_normal
    s_d = mx_kscale(D, 0)
    s_i = mx_kscale(I, 0)
    return {
        "x": (n((G, D, I)) * s_d[:, None]).astype(np.float32),
        "w": (n((D, N)) / np.sqrt(D) / s_d[:, None]).astype(np.float32),
        "ni": (sgn((G, I, 1)) * s_i[:, None]).astype(np.float32),
        "ad": ((np.random.uniform(size=(G, I, J)) < 0.1) * np.random.uniform(0.5, 1.0, (G, I, J)) / 3 / s_i[:, None]).astype(np.float32),
        "bn": (0.5 * n((1, N))).astype(np.float32),
    }


def reference(x, w, ni, ad, bn):
    xq = mxq(f64(x), 1, "e4m3")
    wq = mxq(f64(w), 0, "e4m3")
    z = xq.transpose(0, 2, 1) @ wq
    h = z * f64(ni)
    adq = mxq(f64(ad), 1, "e4m3")
    hq = mxq(h, 1, "e4m3")
    y = adq.transpose(0, 2, 1) @ hq
    out_ = np.maximum(y + f64(bn), 0.0)
    return out_

@@ -1,0 +1,201 @@
+from contextlib import ExitStack
+
+import concourse.mybir as mybir
+
+G, D, I, N, J = 4, 128, 128, 512, 128
+FLOPS = 2 * G * I * N * D + 2 * G * J * N * I
+
+F32 = mybir.dt.float32
+BF16 = mybir.dt.bfloat16
+U32 = mybir.dt.uint32
+U8 = mybir.dt.uint8
+FP8X4 = mybir.dt.float8_e4m3fn_x4
+ACT = mybir.ActivationFunctionType
+ALU = mybir.AluOpType
+
+P = 128
+R = 32
+PACK = 4
+C = 128
+SPAN = 96
+FIRST_ROWS = (0, 64)
+HALF = 2 * C
+
+
+def tile_rows_gnn_gcn_kernel(tc, x, w, ni, ad, bn, out):
+    nc = tc.nc
+    queues = (nc.sync, nc.scalar)
+
+    with ExitStack() as ctx:
+        sb = ctx.enter_context(tc.tile_pool(name="sb", bufs=1))
+        ps = ctx.enter_context(tc.psum_pool(name="ps", bufs=1))
+        ctx.enter_context(tc.manual_schedule())
+
+        x_raw = sb.tile([P, G, PACK * I], F32, align_bytes=64)
+        w_raw = sb.tile([P, 2, PACK * C], F32, align_bytes=64)
+        ad_raw = sb.tile([P, PACK * J], F32, align_bytes=64)
+        ni_sb = sb.tile([P, PACK], F32, align_bytes=64)
+        bn_sb = sb.tile([P, N], F32, align_bytes=64)
+        warm = sb.tile([P, 16], F32, align_bytes=64)
+
+        x_bf = sb.tile([P, PACK, G, R * PACK], BF16, align_bytes=64)
+        w_bf = sb.tile([P, 2, C * PACK], BF16, align_bytes=64)
+        ad_bf = sb.tile([P, J * PACK], BF16, align_bytes=64)
+        h_bf = sb.tile([P, 4, C * PACK], BF16, align_bytes=64)
+
+        x_codes = sb.tile([P, PACK, P], U32, align_bytes=64)
+        x_scales = sb.tile([P, PACK, P], U8, align_bytes=64)
+        w_codes = sb.tile([P, 2, C], U32, align_bytes=64)
+        w_scales = sb.tile([P, 2, C], U8, align_bytes=64)
+        ad_codes = sb.tile([P, J], U32, align_bytes=64)
+        ad_scales = sb.tile([P, J], U8, align_bytes=64)
+        h_codes = sb.tile([P, 4, C], U32, align_bytes=64)
+        h_scales = sb.tile([P, 4, C], U8, align_bytes=64)
+
+        biased = sb.tile([P, G, N], F32, align_bytes=64)
+        result = sb.tile([P, G, N], F32, align_bytes=64)
+
+        z = [ps.tile([P, PACK, C], F32, name="z%d" % c) for c in range(4)]
+        y = [ps.tile([P, N], F32, name="y%d" % g) for g in range(G)]
+
+        def load_w(queue, tile, s):
+            r = FIRST_ROWS[tile]
+            c = 2 * tile + s
+            queue.dma_start(
+                out=w_raw[r : r + R, s, :].rearrange("p (j n) -> p j n", j=PACK),
+                in_=w[:, c * C : (c + 1) * C].rearrange("(p j) n -> p j n", j=PACK),
+            )
+
+        def load_x(queue, tile, g0, g1):
+            r = FIRST_ROWS[tile]
+            queue.dma_start(
+                out=x_raw[r : r + R, g0:g1, :],
+                in_=x[g0:g1].rearrange("g (p j) i -> p g (j i)", j=PACK),
+            )
+
+        def copy(engine, out_ap, in_ap):
+            if engine == "vector":
+                nc.vector.tensor_copy(out=out_ap, in_=in_ap)
+            else:
+                nc.scalar.copy(out=out_ap, in_=in_ap)
+
+        def group_x(engine, g):
+            copy(
+                engine,
+                x_bf[0:SPAN, :, g, :].rearrange("q t (p j) -> q p j t", j=PACK),
+                x_raw[0:SPAN, g, :].rearrange("q (j p t) -> q p j t", j=PACK, t=PACK),
+            )
+
+        def group_rows(engine, out_ap, in_ap):
+            copy(
+                engine,
+                out_ap.rearrange("q (c i j) -> q c j i", i=4, j=PACK),
+                in_ap.rearrange("q (j c i) -> q c j i", i=4, j=PACK),
+            )
+
+        def quantize(codes, scales, values):
+            nc.vector.quantize_mx(out=codes.bitcast(FP8X4), scales=scales, in_=values)
+
+        def project(tile, s, t):
+            r = FIRST_ROWS[tile]
+            nc.tensor.matmul_mx(
+                out=z[2 * tile + s][:, t, :],
+                lhsT=x_codes[r : r + R, t, :].bitcast(FP8X4),
+                lhsT_scale=x_scales[r : r + R, t, :],
+                rhs=w_codes[r : r + R, s, :].bitcast(FP8X4),
+                rhs_scale=w_scales[r : r + R, s, :],
+                start=True,
+                stop=True,
+            )
+
+        def weigh_on_vector(c):
+            nc.vector.tensor_tensor(
+                out=h_bf[:, c, :].rearrange("q (n t) -> q n t", t=PACK),
+                in0=z[c][:].rearrange("q t n -> q n t"),
+                in1=ni_sb[:].unsqueeze(1).to_broadcast([P, C, PACK]),
+                op=ALU.mult,
+            )
+
+        def weigh_on_scalar(c):
+            for t in range(PACK):
+                nc.scalar.activation(
+                    out=h_bf[:, c, :].rearrange("q (n t) -> q t n", t=PACK)[:, t, :],
+                    in_=z[c][:, t, :],
+                    func=ACT.Copy,
+                    scale=ni_sb[:, t : t + 1],
+                )
+
+        def quantize_h(c):
+            quantize(h_codes[:, c, :], h_scales[:, c, :], h_bf[:, c, :])
+
+        def send(g, c):
+            r = g * R
+            nc.tensor.matmul_mx(
+                out=y[g][:, c * C : (c + 1) * C],
+                lhsT=ad_codes[r : r + R, :].bitcast(FP8X4),
+                lhsT_scale=ad_scales[r : r + R, :],
+                rhs=h_codes[r : r + R, c, :].bitcast(FP8X4),
+                rhs_scale=h_scales[r : r + R, c, :],
+                start=True,
+                stop=True,
+            )
+
+        def finish(g, half):
+            cols = slice(half * HALF, (half + 1) * HALF)
+            nc.vector.tensor_tensor(out=biased[:, g, cols], in0=y[g][:, cols], in1=bn_sb[:, cols], op=ALU.add)
+            nc.scalar.activation(out=result[:, g, cols], in_=biased[:, g, cols], func=ACT.Relu)
+            nc.sync.dma_start(out=out[g, :, cols], in_=result[:, g, cols])
+
+        for tile in range(2):
+            load_w(queues[tile], tile, 0)
+        for g0, g1 in ((0, 2), (2, 3), (3, 4)):
+            for tile in range(2):
+                load_x(queues[tile], tile, g0, g1)
+        for tile in range(2):
+            load_w(nc.sync, tile, 1)
+        nc.sync.dma_start(out=ad_raw[:], in_=ad.rearrange("g (p t) j -> (g p) (t j)", t=PACK))
+        nc.sync.dma_start(out=ni_sb[:], in_=ni.rearrange("g (p t) o -> (g p) (t o)", t=PACK))
+        nc.sync.dma_start(out=bn_sb[:], in_=bn[0].partition_broadcast(P))
+
+        nc.vector.memset(warm[:, 0:8], 0.0)
+        nc.scalar.activation(out=warm[:, 8:16], in_=warm[:, 0:8], func=ACT.Relu)
+        nc.vector.memset(w_raw[R : 2 * R, 0, :], 0.0)
+        for g in range(G):
+            nc.vector.memset(x_raw[R : 2 * R, g, :], 0.0)
+        nc.vector.memset(w_raw[R : 2 * R, 1, :], 0.0)
+
+        group_rows("vector", w_bf[0:SPAN, 0, :], w_raw[0:SPAN, 0, :])
+        group_x("vector", 0)
+        group_x("scalar", 1)
+        quantize(w_codes[0:SPAN, 0, :], w_scales[0:SPAN, 0, :], w_bf[0:SPAN, 0, :])
+        group_x("vector", 2)
+        group_x("vector", 3)
+        group_rows("scalar", w_bf[0:SPAN, 1, :], w_raw[0:SPAN, 1, :])
+        group_rows("scalar", ad_bf[:], ad_raw[:])
+        for t in range(PACK):
+            quantize(x_codes[0:SPAN, t, :], x_scales[0:SPAN, t, :], x_bf[0:SPAN, t].rearrange("q g k -> q (g k)"))
+            for tile in range(2):
+                project(tile, 0, t)
+        quantize(w_codes[0:SPAN, 1, :], w_scales[0:SPAN, 1, :], w_bf[0:SPAN, 1, :])
+        for t in range(PACK):
+            for tile in range(2):
+                project(tile, 1, t)
+
+        weigh_on_vector(0)
+        weigh_on_scalar(2)
+        quantize(ad_codes[:], ad_scales[:], ad_bf[:])
+        weigh_on_vector(1)
+        quantize_h(0)
+        quantize_h(1)
+        for c in (0, 1):
+            for g in range(G):
+                send(g, c)
+        weigh_on_vector(3)
+        quantize_h(2)
+        quantize_h(3)
+        for g in range(G):
+            finish(g, 0)
+            for c in (2, 3):
+                send(g, c)
+        for g in range(G):
+            finish(g, 1)

@@ -55,8 +55,10 @@ def tile_rows_gnn_gcn_kernel(tc, x, w, ni, ad, bn, out):
         biased = sb.tile([P, G, N], F32, align_bytes=64)
         result = sb.tile([P, G, N], F32, align_bytes=64)
 
-        z = [ps.tile([P, PACK, C], F32, name="z%d" % c) for c in range(4)]
-        y = [ps.tile([P, N], F32, name="y%d" % g) for g in range(G)]
+        banks = [[ps.tile([P, N], F32, name="bank%d_%d" % (g, h)) for h in range(2)] for g in range(G)]
+
+        def z(c):
+            return banks[2 * (c // 2)][c % 2][:].rearrange("q (t n) -> q t n", t=PACK)
 
         def load_w(queue, tile, s):
             r = FIRST_ROWS[tile]
@@ -99,7 +101,7 @@ def tile_rows_gnn_gcn_kernel(tc, x, w, ni, ad, bn, out):
         def project(tile, s, t):
             r = FIRST_ROWS[tile]
             nc.tensor.matmul_mx(
-                out=z[2 * tile + s][:, t, :],
+                out=z(2 * tile + s)[:, t, :],
                 lhsT=x_codes[r : r + R, t, :].bitcast(FP8X4),
                 lhsT_scale=x_scales[r : r + R, t, :],
                 rhs=w_codes[r : r + R, s, :].bitcast(FP8X4),
@@ -111,7 +113,7 @@ def tile_rows_gnn_gcn_kernel(tc, x, w, ni, ad, bn, out):
         def weigh_on_vector(c):
             nc.vector.tensor_tensor(
                 out=h_bf[:, c, :].rearrange("q (n t) -> q n t", t=PACK),
-                in0=z[c][:].rearrange("q t n -> q n t"),
+                in0=z(c).rearrange("q t n -> q n t"),
                 in1=ni_sb[:].unsqueeze(1).to_broadcast([P, C, PACK]),
                 op=ALU.mult,
             )
@@ -120,7 +122,7 @@ def tile_rows_gnn_gcn_kernel(tc, x, w, ni, ad, bn, out):
             for t in range(PACK):
                 nc.scalar.activation(
                     out=h_bf[:, c, :].rearrange("q (n t) -> q t n", t=PACK)[:, t, :],
-                    in_=z[c][:, t, :],
+                    in_=z(c)[:, t, :],
                     func=ACT.Copy,
                     scale=ni_sb[:, t : t + 1],
                 )
@@ -131,7 +133,7 @@ def tile_rows_gnn_gcn_kernel(tc, x, w, ni, ad, bn, out):
         def send(g, c):
             r = g * R
             nc.tensor.matmul_mx(
-                out=y[g][:, c * C : (c + 1) * C],
+                out=banks[g][c // 2][:, (c % 2) * C : (c % 2 + 1) * C],
                 lhsT=ad_codes[r : r + R, :].bitcast(FP8X4),
                 lhsT_scale=ad_scales[r : r + R, :],
                 rhs=h_codes[r : r + R, c, :].bitcast(FP8X4),
@@ -142,7 +144,7 @@ def tile_rows_gnn_gcn_kernel(tc, x, w, ni, ad, bn, out):
 
         def finish(g, half):
             cols = slice(half * HALF, (half + 1) * HALF)
-            nc.vector.tensor_tensor(out=biased[:, g, cols], in0=y[g][:, cols], in1=bn_sb[:, cols], op=ALU.add)
+            nc.vector.tensor_tensor(out=biased[:, g, cols], in0=banks[g][half][:, 0:HALF], in1=bn_sb[:, cols], op=ALU.add)
             nc.scalar.activation(out=result[:, g, cols], in_=biased[:, g, cols], func=ACT.Relu)
             nc.sync.dma_start(out=out[g, :, cols], in_=result[:, g, cols])
 
@@ -167,9 +169,9 @@ def tile_rows_gnn_gcn_kernel(tc, x, w, ni, ad, bn, out):
         group_rows("vector", w_bf[0:SPAN, 0, :], w_raw[0:SPAN, 0, :])
         group_x("vector", 0)
         group_x("scalar", 1)
-        quantize(w_codes[0:SPAN, 0, :], w_scales[0:SPAN, 0, :], w_bf[0:SPAN, 0, :])
         group_x("vector", 2)
         group_x("vector", 3)
+        quantize(w_codes[0:SPAN, 0, :], w_scales[0:SPAN, 0, :], w_bf[0:SPAN, 0, :])
         group_rows("scalar", w_bf[0:SPAN, 1, :], w_raw[0:SPAN, 1, :])
         group_rows("scalar", ad_bf[:], ad_raw[:])
         for t in range(PACK):
@@ -183,19 +185,23 @@ def tile_rows_gnn_gcn_kernel(tc, x, w, ni, ad, bn, out):
 
         weigh_on_vector(0)
         weigh_on_scalar(2)
-        quantize(ad_codes[:], ad_scales[:], ad_bf[:])
         weigh_on_vector(1)
+        quantize(ad_codes[:], ad_scales[:], ad_bf[:])
         quantize_h(0)
         quantize_h(1)
         for c in (0, 1):
-            for g in range(G):
+            for g in (0, 1, 3):
                 send(g, c)
+        for c in (0, 1):
+            send(2, c)
         weigh_on_vector(3)
         quantize_h(2)
+        finish(0, 0)
         quantize_h(3)
-        for g in range(G):
-            finish(g, 0)
-            for c in (2, 3):
+        for c in (2, 3):
+            for g in range(G):
                 send(g, c)
+        for g in (1, 3, 2):
+            finish(g, 0)
         for g in range(G):
             finish(g, 1)

@@ -142,9 +142,9 @@ def tile_rows_gnn_gcn_kernel(tc, x, w, ni, ad, bn, out):
                 stop=True,
             )
 
-        def finish(g, half):
-            cols = slice(half * HALF, (half + 1) * HALF)
-            nc.vector.tensor_tensor(out=biased[:, g, cols], in0=banks[g][half][:, 0:HALF], in1=bn_sb[:, cols], op=ALU.add)
+        def finish(g, half, n0=0, n1=HALF):
+            cols = slice(half * HALF + n0, half * HALF + n1)
+            nc.vector.tensor_tensor(out=biased[:, g, cols], in0=banks[g][half][:, n0:n1], in1=bn_sb[:, cols], op=ALU.add)
             nc.scalar.activation(out=result[:, g, cols], in_=biased[:, g, cols], func=ACT.Relu)
             nc.sync.dma_start(out=out[g, :, cols], in_=result[:, g, cols])
 
@@ -185,8 +185,8 @@ def tile_rows_gnn_gcn_kernel(tc, x, w, ni, ad, bn, out):
 
         weigh_on_vector(0)
         weigh_on_scalar(2)
-        weigh_on_vector(1)
         quantize(ad_codes[:], ad_scales[:], ad_bf[:])
+        weigh_on_vector(1)
         quantize_h(0)
         quantize_h(1)
         for c in (0, 1):
@@ -203,5 +203,7 @@ def tile_rows_gnn_gcn_kernel(tc, x, w, ni, ad, bn, out):
                 send(g, c)
         for g in (1, 3, 2):
             finish(g, 0)
-        for g in range(G):
+        for g in range(G - 1):
             finish(g, 1)
+        finish(G - 1, 1, 0, C)
+        finish(G - 1, 1, C, HALF)

@@ -7,6 +7,7 @@ FLOPS = 2 * G * I * N * D + 2 * G * J * N * I
 
 F32 = mybir.dt.float32
 BF16 = mybir.dt.bfloat16
+I32 = mybir.dt.int32
 U32 = mybir.dt.uint32
 U8 = mybir.dt.uint8
 FP8X4 = mybir.dt.float8_e4m3fn_x4
@@ -20,6 +21,7 @@ C = 128
 SPAN = 96
 FIRST_ROWS = (0, 64)
 HALF = 2 * C
+EARLY = 64
 
 
 def tile_rows_gnn_gcn_kernel(tc, x, w, ni, ad, bn, out):
@@ -36,7 +38,6 @@ def tile_rows_gnn_gcn_kernel(tc, x, w, ni, ad, bn, out):
         ad_raw = sb.tile([P, PACK * J], F32, align_bytes=64)
         ni_sb = sb.tile([P, PACK], F32, align_bytes=64)
         bn_sb = sb.tile([P, N], F32, align_bytes=64)
-        warm = sb.tile([P, 16], F32, align_bytes=64)
 
         x_bf = sb.tile([P, PACK, G, R * PACK], BF16, align_bytes=64)
         w_bf = sb.tile([P, 2, C * PACK], BF16, align_bytes=64)
@@ -159,12 +160,10 @@ def tile_rows_gnn_gcn_kernel(tc, x, w, ni, ad, bn, out):
         nc.sync.dma_start(out=ni_sb[:], in_=ni.rearrange("g (p t) o -> (g p) (t o)", t=PACK))
         nc.sync.dma_start(out=bn_sb[:], in_=bn[0].partition_broadcast(P))
 
-        nc.vector.memset(warm[:, 0:8], 0.0)
-        nc.scalar.activation(out=warm[:, 8:16], in_=warm[:, 0:8], func=ACT.Relu)
-        nc.vector.memset(w_raw[R : 2 * R, 0, :], 0.0)
-        for g in range(G):
-            nc.vector.memset(x_raw[R : 2 * R, g, :], 0.0)
-        nc.vector.memset(w_raw[R : 2 * R, 1, :], 0.0)
+        nc.vector.memset(w_raw[R : 2 * R, 0, :].bitcast(I32), 0)
+        nc.scalar.activation(out=w_raw[R : 2 * R, 1, 0:EARLY], in_=w_raw[R : 2 * R, 0, 0:EARLY], func=ACT.Relu)
+        nc.vector.memset(x_raw[R : 2 * R].rearrange("q g k -> q (g k)").bitcast(I32), 0)
+        nc.vector.memset(w_raw[R : 2 * R, 1, EARLY:].bitcast(I32), 0)
 
         group_rows("vector", w_bf[0:SPAN, 0, :], w_raw[0:SPAN, 0, :])
         group_x("vector", 0)

@@ -21,7 +21,8 @@ C = 128
 SPAN = 96
 FIRST_ROWS = (0, 64)
 HALF = 2 * C
-EARLY = 64
+F32_MAX = 3.4028234663852886e38
+EARLY = 16
 
 
 def tile_rows_gnn_gcn_kernel(tc, x, w, ni, ad, bn, out):
@@ -143,10 +144,20 @@ def tile_rows_gnn_gcn_kernel(tc, x, w, ni, ad, bn, out):
                 stop=True,
             )
 
-        def finish(g, half, n0=0, n1=HALF):
-            cols = slice(half * HALF + n0, half * HALF + n1)
-            nc.vector.tensor_tensor(out=biased[:, g, cols], in0=banks[g][half][:, n0:n1], in1=bn_sb[:, cols], op=ALU.add)
-            nc.scalar.activation(out=result[:, g, cols], in_=biased[:, g, cols], func=ACT.Relu)
+        def finish(g, half, clip="scalar"):
+            cols = slice(half * HALF, (half + 1) * HALF)
+            nc.vector.tensor_tensor(out=biased[:, g, cols], in0=banks[g][half][:, 0:HALF], in1=bn_sb[:, cols], op=ALU.add)
+            if clip == "scalar":
+                nc.scalar.activation(out=result[:, g, cols], in_=biased[:, g, cols], func=ACT.Relu)
+            else:
+                nc.gpsimd.tensor_scalar(
+                    out=result[:, g, cols],
+                    in0=biased[:, g, cols],
+                    scalar1=F32_MAX,
+                    scalar2=0.0,
+                    op0=ALU.min,
+                    op1=ALU.max,
+                )
             nc.sync.dma_start(out=out[g, :, cols], in_=result[:, g, cols])
 
         for tile in range(2):
@@ -160,8 +171,9 @@ def tile_rows_gnn_gcn_kernel(tc, x, w, ni, ad, bn, out):
         nc.sync.dma_start(out=ni_sb[:], in_=ni.rearrange("g (p t) o -> (g p) (t o)", t=PACK))
         nc.sync.dma_start(out=bn_sb[:], in_=bn[0].partition_broadcast(P))
 
-        nc.vector.memset(w_raw[R : 2 * R, 0, :].bitcast(I32), 0)
+        nc.vector.memset(w_raw[R : 2 * R, 0, 0:EARLY].bitcast(I32), 0)
         nc.scalar.activation(out=w_raw[R : 2 * R, 1, 0:EARLY], in_=w_raw[R : 2 * R, 0, 0:EARLY], func=ACT.Relu)
+        nc.vector.memset(w_raw[R : 2 * R, 0, EARLY:].bitcast(I32), 0)
         nc.vector.memset(x_raw[R : 2 * R].rearrange("q g k -> q (g k)").bitcast(I32), 0)
         nc.vector.memset(w_raw[R : 2 * R, 1, EARLY:].bitcast(I32), 0)
 
@@ -178,8 +190,8 @@ def tile_rows_gnn_gcn_kernel(tc, x, w, ni, ad, bn, out):
             for tile in range(2):
                 project(tile, 0, t)
         quantize(w_codes[0:SPAN, 1, :], w_scales[0:SPAN, 1, :], w_bf[0:SPAN, 1, :])
-        for t in range(PACK):
-            for tile in range(2):
+        for tile in range(2):
+            for t in range(PACK):
                 project(tile, 1, t)
 
         weigh_on_vector(0)
@@ -202,7 +214,5 @@ def tile_rows_gnn_gcn_kernel(tc, x, w, ni, ad, bn, out):
                 send(g, c)
         for g in (1, 3, 2):
             finish(g, 0)
-        for g in range(G - 1):
-            finish(g, 1)
-        finish(G - 1, 1, 0, C)
-        finish(G - 1, 1, C, HALF)
+        for g in range(G):
+            finish(g, 1, clip="gpsimd" if g % 2 == 0 else "scalar")

@@ -7,7 +7,6 @@ FLOPS = 2 * G * I * N * D + 2 * G * J * N * I
 
 F32 = mybir.dt.float32
 BF16 = mybir.dt.bfloat16
-I32 = mybir.dt.int32
 U32 = mybir.dt.uint32
 U8 = mybir.dt.uint8
 FP8X4 = mybir.dt.float8_e4m3fn_x4
@@ -21,7 +20,6 @@ C = 128
 SPAN = 96
 FIRST_ROWS = (0, 64)
 HALF = 2 * C
-F32_MAX = 3.4028234663852886e38
 EARLY = 16
 
 
@@ -34,28 +32,28 @@ def tile_rows_gnn_gcn_kernel(tc, x, w, ni, ad, bn, out):
         ps = ctx.enter_context(tc.psum_pool(name="ps", bufs=1))
         ctx.enter_context(tc.manual_schedule())
 
-        x_raw = sb.tile([P, G, PACK * I], F32, align_bytes=64)
-        w_raw = sb.tile([P, 2, PACK * C], F32, align_bytes=64)
-        ad_raw = sb.tile([P, PACK * J], F32, align_bytes=64)
-        ni_sb = sb.tile([P, PACK], F32, align_bytes=64)
-        bn_sb = sb.tile([P, N], F32, align_bytes=64)
+        x_raw = sb.tile([P, G, PACK * I], F32, align_bytes=256)
+        w_raw = sb.tile([P, 2, PACK * C], F32, align_bytes=256)
+        ad_raw = sb.tile([P, PACK * J], F32, align_bytes=256)
+        bn_sb = sb.tile([P, N], F32, align_bytes=256)
+        ni_sb = sb.tile([P, PACK], F32, align_bytes=128)
 
-        x_bf = sb.tile([P, PACK, G, R * PACK], BF16, align_bytes=64)
-        w_bf = sb.tile([P, 2, C * PACK], BF16, align_bytes=64)
-        ad_bf = sb.tile([P, J * PACK], BF16, align_bytes=64)
-        h_bf = sb.tile([P, 4, C * PACK], BF16, align_bytes=64)
+        x_bf = sb.tile([P, PACK, G, R * PACK], BF16, align_bytes=128)
+        w_bf = sb.tile([P, 2, C * PACK], BF16, align_bytes=128)
+        ad_bf = sb.tile([P, J * PACK], BF16, align_bytes=128)
+        h_bf = sb.tile([P, 4, C * PACK], BF16, align_bytes=128)
 
-        x_codes = sb.tile([P, PACK, P], U32, align_bytes=64)
-        x_scales = sb.tile([P, PACK, P], U8, align_bytes=64)
-        w_codes = sb.tile([P, 2, C], U32, align_bytes=64)
-        w_scales = sb.tile([P, 2, C], U8, align_bytes=64)
-        ad_codes = sb.tile([P, J], U32, align_bytes=64)
-        ad_scales = sb.tile([P, J], U8, align_bytes=64)
-        h_codes = sb.tile([P, 4, C], U32, align_bytes=64)
-        h_scales = sb.tile([P, 4, C], U8, align_bytes=64)
+        x_codes = sb.tile([P, PACK, P], U32, align_bytes=128)
+        x_scales = sb.tile([P, PACK, P], U8, align_bytes=128)
+        w_codes = sb.tile([P, 2, C], U32, align_bytes=128)
+        w_scales = sb.tile([P, 2, C], U8, align_bytes=128)
+        ad_codes = sb.tile([P, J], U32, align_bytes=128)
+        ad_scales = sb.tile([P, J], U8, align_bytes=128)
+        h_codes = sb.tile([P, 4, C], U32, align_bytes=128)
+        h_scales = sb.tile([P, 4, C], U8, align_bytes=128)
 
-        biased = sb.tile([P, G, N], F32, align_bytes=64)
-        result = sb.tile([P, G, N], F32, align_bytes=64)
+        biased = sb.tile([P, G, N], F32, align_bytes=256)
+        result = sb.tile([P, G, N], F32, align_bytes=256)
 
         banks = [[ps.tile([P, N], F32, name="bank%d_%d" % (g, h)) for h in range(2)] for g in range(G)]
 
@@ -144,20 +142,10 @@ def tile_rows_gnn_gcn_kernel(tc, x, w, ni, ad, bn, out):
                 stop=True,
             )
 
-        def finish(g, half, clip="scalar"):
+        def finish(g, half):
             cols = slice(half * HALF, (half + 1) * HALF)
             nc.vector.tensor_tensor(out=biased[:, g, cols], in0=banks[g][half][:, 0:HALF], in1=bn_sb[:, cols], op=ALU.add)
-            if clip == "scalar":
-                nc.scalar.activation(out=result[:, g, cols], in_=biased[:, g, cols], func=ACT.Relu)
-            else:
-                nc.gpsimd.tensor_scalar(
-                    out=result[:, g, cols],
-                    in0=biased[:, g, cols],
-                    scalar1=F32_MAX,
-                    scalar2=0.0,
-                    op0=ALU.min,
-                    op1=ALU.max,
-                )
+            nc.scalar.activation(out=result[:, g, cols], in_=biased[:, g, cols], func=ACT.Relu)
             nc.sync.dma_start(out=out[g, :, cols], in_=result[:, g, cols])
 
         for tile in range(2):
@@ -171,11 +159,12 @@ def tile_rows_gnn_gcn_kernel(tc, x, w, ni, ad, bn, out):
         nc.sync.dma_start(out=ni_sb[:], in_=ni.rearrange("g (p t) o -> (g p) (t o)", t=PACK))
         nc.sync.dma_start(out=bn_sb[:], in_=bn[0].partition_broadcast(P))
 
-        nc.vector.memset(w_raw[R : 2 * R, 0, 0:EARLY].bitcast(I32), 0)
+        nc.vector.memset(w_raw[R : 2 * R, 0, 0:EARLY], 0.0)
         nc.scalar.activation(out=w_raw[R : 2 * R, 1, 0:EARLY], in_=w_raw[R : 2 * R, 0, 0:EARLY], func=ACT.Relu)
-        nc.vector.memset(w_raw[R : 2 * R, 0, EARLY:].bitcast(I32), 0)
-        nc.vector.memset(x_raw[R : 2 * R].rearrange("q g k -> q (g k)").bitcast(I32), 0)
-        nc.vector.memset(w_raw[R : 2 * R, 1, EARLY:].bitcast(I32), 0)
+        nc.vector.memset(w_raw[R : 2 * R, 0, EARLY:], 0.0)
+        for g in range(G):
+            nc.vector.memset(x_raw[R : 2 * R, g, :], 0.0)
+        nc.vector.memset(w_raw[R : 2 * R, 1, EARLY:], 0.0)
 
         group_rows("vector", w_bf[0:SPAN, 0, :], w_raw[0:SPAN, 0, :])
         group_x("vector", 0)
@@ -215,4 +204,4 @@ def tile_rows_gnn_gcn_kernel(tc, x, w, ni, ad, bn, out):
         for g in (1, 3, 2):
             finish(g, 0)
         for g in range(G):
-            finish(g, 1, clip="gpsimd" if g % 2 == 0 else "scalar")
+            finish(g, 1)

@@ -40,7 +40,6 @@ def tile_rows_gnn_gcn_kernel(tc, x, w, ni, ad, bn, out):
 
         x_bf = sb.tile([P, PACK, G, R * PACK], BF16, align_bytes=128)
         w_bf = sb.tile([P, 2, C * PACK], BF16, align_bytes=128)
-        ad_bf = sb.tile([P, J * PACK], BF16, align_bytes=128)
         h_bf = sb.tile([P, 4, C * PACK], BF16, align_bytes=128)
 
         x_codes = sb.tile([P, PACK, P], U32, align_bytes=128)
@@ -173,21 +172,29 @@ def tile_rows_gnn_gcn_kernel(tc, x, w, ni, ad, bn, out):
         group_x("vector", 3)
         quantize(w_codes[0:SPAN, 0, :], w_scales[0:SPAN, 0, :], w_bf[0:SPAN, 0, :])
         group_rows("scalar", w_bf[0:SPAN, 1, :], w_raw[0:SPAN, 1, :])
-        group_rows("scalar", ad_bf[:], ad_raw[:])
         for t in range(PACK):
             quantize(x_codes[0:SPAN, t, :], x_scales[0:SPAN, t, :], x_bf[0:SPAN, t].rearrange("q g k -> q (g k)"))
             for tile in range(2):
                 project(tile, 0, t)
         quantize(w_codes[0:SPAN, 1, :], w_scales[0:SPAN, 1, :], w_bf[0:SPAN, 1, :])
+        ad_bf = w_bf[:, 1, :]
+        nc.gpsimd.tensor_scalar(
+            out=ad_bf.rearrange("q (n j) -> q n j", j=PACK),
+            in0=ad_raw[:].rearrange("q (j n) -> q n j", j=PACK),
+            scalar1=1.0,
+            scalar2=0.0,
+            op0=ALU.mult,
+            op1=ALU.add,
+        )
         for tile in range(2):
             for t in range(PACK):
                 project(tile, 1, t)
 
         weigh_on_vector(0)
         weigh_on_scalar(2)
-        quantize(ad_codes[:], ad_scales[:], ad_bf[:])
         weigh_on_vector(1)
         quantize_h(0)
+        quantize(ad_codes[:], ad_scales[:], ad_bf)
         quantize_h(1)
         for c in (0, 1):
             for g in (0, 1, 3):

@@ -19,8 +19,9 @@ PACK = 4
 C = 128
 SPAN = 96
 FIRST_ROWS = (0, 64)
-HALF = 2 * C
 EARLY = 16
+SEEDS = 16
+SHARE = 64
 
 
 def tile_rows_gnn_gcn_kernel(tc, x, w, ni, ad, bn, out):
@@ -35,12 +36,15 @@ def tile_rows_gnn_gcn_kernel(tc, x, w, ni, ad, bn, out):
         x_raw = sb.tile([P, G, PACK * I], F32, align_bytes=256)
         w_raw = sb.tile([P, 2, PACK * C], F32, align_bytes=256)
         ad_raw = sb.tile([P, PACK * J], F32, align_bytes=256)
+        bn_seed = sb.tile([P, N], F32, align_bytes=256)
         bn_sb = sb.tile([P, N], F32, align_bytes=256)
         ni_sb = sb.tile([P, PACK], F32, align_bytes=128)
 
         x_bf = sb.tile([P, PACK, G, R * PACK], BF16, align_bytes=128)
         w_bf = sb.tile([P, 2, C * PACK], BF16, align_bytes=128)
+        ad_bf = sb.tile([P, J * PACK], BF16, align_bytes=128)
         h_bf = sb.tile([P, 4, C * PACK], BF16, align_bytes=128)
+        h_rows = sb.tile([P, 2, C * PACK], BF16, align_bytes=128)
 
         x_codes = sb.tile([P, PACK, P], U32, align_bytes=128)
         x_scales = sb.tile([P, PACK, P], U8, align_bytes=128)
@@ -54,14 +58,26 @@ def tile_rows_gnn_gcn_kernel(tc, x, w, ni, ad, bn, out):
         biased = sb.tile([P, G, N], F32, align_bytes=256)
         result = sb.tile([P, G, N], F32, align_bytes=256)
 
-        banks = [[ps.tile([P, N], F32, name="bank%d_%d" % (g, h)) for h in range(2)] for g in range(G)]
+        banks0 = [ps.tile([P, N], F32, name="tile0_%d" % k) for k in range(2)]
+        banks2 = [ps.tile([P, N], F32, name="tile2_%d" % k) for k in range(PACK)]
+        bank1 = ps.tile([P, N], F32)
+        bank3 = ps.tile([P, N], F32)
 
-        def z(c):
-            return banks[2 * (c // 2)][c % 2][:].rearrange("q (t n) -> q t n", t=PACK)
+        def z(c, t):
+            if c % 2 == 0:
+                return banks0[c // 2][:, t * C : (t + 1) * C]
+            return banks2[t][:, (c // 2) * C : (c // 2 + 1) * C]
+
+        def y(g, c0, c1):
+            if g == 0:
+                return banks0[c0 // 2][:, c0 * C : c1 * C]
+            if g == 2:
+                return banks2[c0 // 2][:, (2 + c0 % 2) * C : (2 + c0 % 2 + c1 - c0) * C]
+            return (bank1 if g == 1 else bank3)[:, c0 * C : c1 * C]
 
         def load_w(queue, tile, s):
             r = FIRST_ROWS[tile]
-            c = 2 * tile + s
+            c = 2 * s + tile
             queue.dma_start(
                 out=w_raw[r : r + R, s, :].rearrange("p (j n) -> p j n", j=PACK),
                 in_=w[:, c * C : (c + 1) * C].rearrange("(p j) n -> p j n", j=PACK),
@@ -94,13 +110,20 @@ def tile_rows_gnn_gcn_kernel(tc, x, w, ni, ad, bn, out):
                 in_ap.rearrange("q (j c i) -> q c j i", i=4, j=PACK),
             )
 
+        def group_h(engine, c, n0, n1):
+            copy(
+                engine,
+                h_bf[:, c, :].rearrange("q (c i t) -> q c t i", i=4, t=PACK)[:, n0 // 4 : n1 // 4],
+                h_rows[:, c // 2, :].rearrange("q (t c i) -> q c t i", i=4, t=PACK)[:, n0 // 4 : n1 // 4],
+            )
+
         def quantize(codes, scales, values):
             nc.vector.quantize_mx(out=codes.bitcast(FP8X4), scales=scales, in_=values)
 
         def project(tile, s, t):
             r = FIRST_ROWS[tile]
             nc.tensor.matmul_mx(
-                out=z(2 * tile + s)[:, t, :],
+                out=z(2 * s + tile, t),
                 lhsT=x_codes[r : r + R, t, :].bitcast(FP8X4),
                 lhsT_scale=x_scales[r : r + R, t, :],
                 rhs=w_codes[r : r + R, s, :].bitcast(FP8X4),
@@ -109,22 +132,21 @@ def tile_rows_gnn_gcn_kernel(tc, x, w, ni, ad, bn, out):
                 stop=True,
             )
 
-        def weigh_on_vector(c):
+        def weigh_on_vector(c, n0, n1):
             nc.vector.tensor_tensor(
-                out=h_bf[:, c, :].rearrange("q (n t) -> q n t", t=PACK),
-                in0=z(c).rearrange("q t n -> q n t"),
-                in1=ni_sb[:].unsqueeze(1).to_broadcast([P, C, PACK]),
+                out=h_bf[:, c, :].rearrange("q (n t) -> q n t", t=PACK)[:, n0:n1],
+                in0=banks0[c // 2][:].rearrange("q (t n) -> q n t", t=PACK)[:, n0:n1],
+                in1=ni_sb[:].unsqueeze(1).to_broadcast([P, n1 - n0, PACK]),
                 op=ALU.mult,
             )
 
-        def weigh_on_scalar(c):
-            for t in range(PACK):
-                nc.scalar.activation(
-                    out=h_bf[:, c, :].rearrange("q (n t) -> q t n", t=PACK)[:, t, :],
-                    in_=z(c)[:, t, :],
-                    func=ACT.Copy,
-                    scale=ni_sb[:, t : t + 1],
-                )
+        def weigh_on_scalar(c, t):
+            nc.scalar.activation(
+                out=h_rows[:, c // 2, t * C : (t + 1) * C],
+                in_=z(c, t),
+                func=ACT.Copy,
+                scale=ni_sb[:, t : t + 1],
+            )
 
         def quantize_h(c):
             quantize(h_codes[:, c, :], h_scales[:, c, :], h_bf[:, c, :])
@@ -132,7 +154,7 @@ def tile_rows_gnn_gcn_kernel(tc, x, w, ni, ad, bn, out):
         def send(g, c):
             r = g * R
             nc.tensor.matmul_mx(
-                out=banks[g][c // 2][:, (c % 2) * C : (c % 2 + 1) * C],
+                out=y(g, c, c + 1),
                 lhsT=ad_codes[r : r + R, :].bitcast(FP8X4),
                 lhsT_scale=ad_scales[r : r + R, :],
                 rhs=h_codes[r : r + R, c, :].bitcast(FP8X4),
@@ -141,9 +163,9 @@ def tile_rows_gnn_gcn_kernel(tc, x, w, ni, ad, bn, out):
                 stop=True,
             )
 
-        def finish(g, half):
-            cols = slice(half * HALF, (half + 1) * HALF)
-            nc.vector.tensor_tensor(out=biased[:, g, cols], in0=banks[g][half][:, 0:HALF], in1=bn_sb[:, cols], op=ALU.add)
+        def finish(g, c0, c1):
+            cols = slice(c0 * C, c1 * C)
+            nc.vector.tensor_tensor(out=biased[:, g, cols], in0=y(g, c0, c1), in1=bn_sb[:, cols], op=ALU.add)
             nc.scalar.activation(out=result[:, g, cols], in_=biased[:, g, cols], func=ACT.Relu)
             nc.sync.dma_start(out=out[g, :, cols], in_=result[:, g, cols])
 
@@ -154,9 +176,15 @@ def tile_rows_gnn_gcn_kernel(tc, x, w, ni, ad, bn, out):
                 load_x(queues[tile], tile, g0, g1)
         for tile in range(2):
             load_w(nc.sync, tile, 1)
-        nc.sync.dma_start(out=ad_raw[:], in_=ad.rearrange("g (p t) j -> (g p) (t j)", t=PACK))
         nc.sync.dma_start(out=ni_sb[:], in_=ni.rearrange("g (p t) o -> (g p) (t o)", t=PACK))
-        nc.sync.dma_start(out=bn_sb[:], in_=bn[0].partition_broadcast(P))
+        nc.sync.dma_start(out=ad_raw[:], in_=ad.rearrange("g (p t) j -> (g p) (t j)", t=PACK))
+        seeds = bn_seed[R : R + 4 * SEEDS : 4, :]
+        nc.sync.dma_start(out=seeds, in_=bn[0].partition_broadcast(SEEDS))
+        for c0, c1 in ((0, 2 * C), (2 * C, N)):
+            nc.sync.dma_start(
+                out=bn_sb[:, c0:c1],
+                in_=seeds[:, c0:c1].unsqueeze(1).to_broadcast([SEEDS, P // SEEDS, c1 - c0]),
+            )
 
         nc.vector.memset(w_raw[R : 2 * R, 0, 0:EARLY], 0.0)
         nc.scalar.activation(out=w_raw[R : 2 * R, 1, 0:EARLY], in_=w_raw[R : 2 * R, 0, 0:EARLY], func=ACT.Relu)
@@ -176,39 +204,38 @@ def tile_rows_gnn_gcn_kernel(tc, x, w, ni, ad, bn, out):
             quantize(x_codes[0:SPAN, t, :], x_scales[0:SPAN, t, :], x_bf[0:SPAN, t].rearrange("q g k -> q (g k)"))
             for tile in range(2):
                 project(tile, 0, t)
+        group_rows("vector", ad_bf[:], ad_raw[:])
         quantize(w_codes[0:SPAN, 1, :], w_scales[0:SPAN, 1, :], w_bf[0:SPAN, 1, :])
-        ad_bf = w_bf[:, 1, :]
-        nc.gpsimd.tensor_scalar(
-            out=ad_bf.rearrange("q (n j) -> q n j", j=PACK),
-            in0=ad_raw[:].rearrange("q (j n) -> q n j", j=PACK),
-            scalar1=1.0,
-            scalar2=0.0,
-            op0=ALU.mult,
-            op1=ALU.add,
-        )
+        for t in range(PACK):
+            weigh_on_scalar(1, t)
         for tile in range(2):
             for t in range(PACK):
                 project(tile, 1, t)
 
-        weigh_on_vector(0)
-        weigh_on_scalar(2)
-        weigh_on_vector(1)
+        weigh_on_vector(0, 0, C)
+        group_h("scalar", 1, SHARE, C)
+        quantize(ad_codes[:], ad_scales[:], ad_bf[:])
+        group_h("vector", 1, 0, SHARE)
         quantize_h(0)
-        quantize(ad_codes[:], ad_scales[:], ad_bf)
         quantize_h(1)
+        for t in range(PACK):
+            weigh_on_scalar(3, t)
         for c in (0, 1):
-            for g in (0, 1, 3):
+            for g in (1, 3, 0):
                 send(g, c)
         for c in (0, 1):
             send(2, c)
-        weigh_on_vector(3)
+        group_h("scalar", 3, SHARE, C)
+        weigh_on_vector(2, 0, C)
+        group_h("vector", 3, 0, SHARE)
+        finish(1, 0, 2)
         quantize_h(2)
-        finish(0, 0)
         quantize_h(3)
-        for c in (2, 3):
-            for g in range(G):
+        finish(3, 0, 2)
+        finish(0, 0, 2)
+        finish(2, 0, 2)
+        for g in (1, 3, 0, 2):
+            for c in (2, 3):
                 send(g, c)
-        for g in (1, 3, 2):
-            finish(g, 0)
-        for g in range(G):
-            finish(g, 1)
+        for g in (1, 3, 0, 2):
+            finish(g, 2, 4)

@@ -96,11 +96,11 @@ def tile_rows_gnn_gcn_kernel(tc, x, w, ni, ad, bn, out):
             else:
                 nc.scalar.copy(out=out_ap, in_=in_ap)
 
-        def group_x(engine, g):
+        def group_x(engine, g, t0, t1):
             copy(
                 engine,
-                x_bf[0:SPAN, :, g, :].rearrange("q t (p j) -> q p j t", j=PACK),
-                x_raw[0:SPAN, g, :].rearrange("q (j p t) -> q p j t", j=PACK, t=PACK),
+                x_bf[0:SPAN, t0:t1, g, :].rearrange("q t (p j) -> q p j t", j=PACK),
+                x_raw[0:SPAN, g, :].rearrange("q (j p t) -> q p j t", j=PACK, t=PACK)[:, :, :, t0:t1],
             )
 
         def group_rows(engine, out_ap, in_ap):
@@ -176,8 +176,8 @@ def tile_rows_gnn_gcn_kernel(tc, x, w, ni, ad, bn, out):
                 load_x(queues[tile], tile, g0, g1)
         for tile in range(2):
             load_w(nc.sync, tile, 1)
-        nc.sync.dma_start(out=ni_sb[:], in_=ni.rearrange("g (p t) o -> (g p) (t o)", t=PACK))
         nc.sync.dma_start(out=ad_raw[:], in_=ad.rearrange("g (p t) j -> (g p) (t j)", t=PACK))
+        nc.sync.dma_start(out=ni_sb[:], in_=ni.rearrange("g (p t) o -> (g p) (t o)", t=PACK))
         seeds = bn_seed[R : R + 4 * SEEDS : 4, :]
         nc.sync.dma_start(out=seeds, in_=bn[0].partition_broadcast(SEEDS))
         for c0, c1 in ((0, 2 * C), (2 * C, N)):
@@ -194,10 +194,11 @@ def tile_rows_gnn_gcn_kernel(tc, x, w, ni, ad, bn, out):
         nc.vector.memset(w_raw[R : 2 * R, 1, EARLY:], 0.0)
 
         group_rows("vector", w_bf[0:SPAN, 0, :], w_raw[0:SPAN, 0, :])
-        group_x("vector", 0)
-        group_x("scalar", 1)
-        group_x("vector", 2)
-        group_x("vector", 3)
+        group_x("vector", 0, 0, PACK)
+        group_x("scalar", 1, 0, PACK)
+        group_x("vector", 2, 0, PACK)
+        group_x("vector", 3, 0, 2)
+        group_x("scalar", 3, 2, PACK)
         quantize(w_codes[0:SPAN, 0, :], w_scales[0:SPAN, 0, :], w_bf[0:SPAN, 0, :])
         group_rows("scalar", w_bf[0:SPAN, 1, :], w_raw[0:SPAN, 1, :])
         for t in range(PACK):
@@ -214,8 +215,8 @@ def tile_rows_gnn_gcn_kernel(tc, x, w, ni, ad, bn, out):
 
         weigh_on_vector(0, 0, C)
         group_h("scalar", 1, SHARE, C)
-        quantize(ad_codes[:], ad_scales[:], ad_bf[:])
         group_h("vector", 1, 0, SHARE)
+        quantize(ad_codes[:], ad_scales[:], ad_bf[:])
         quantize_h(0)
         quantize_h(1)
         for t in range(PACK):

from contextlib import ExitStack

import concourse.mybir as mybir

G, D, I, N, J = 4, 128, 128, 512, 128
FLOPS = 2 * G * I * N * D + 2 * G * J * N * I

F32 = mybir.dt.float32
BF16 = mybir.dt.bfloat16
U32 = mybir.dt.uint32
U8 = mybir.dt.uint8
FP8X4 = mybir.dt.float8_e4m3fn_x4
ACT = mybir.ActivationFunctionType
ALU = mybir.AluOpType

P = 128
R = 32
PACK = 4
C = 128
SPAN = 96
FIRST_ROWS = (0, 64)
EARLY = 16
SEEDS = 16
SHARE = 64


def tile_rows_gnn_gcn_kernel(tc, x, w, ni, ad, bn, out):
    nc = tc.nc
    queues = (nc.sync, nc.scalar)

    with ExitStack() as ctx:
        sb = ctx.enter_context(tc.tile_pool(name="sb", bufs=1))
        ps = ctx.enter_context(tc.psum_pool(name="ps", bufs=1))
        ctx.enter_context(tc.manual_schedule())

        x_raw = sb.tile([P, G, PACK * I], F32, align_bytes=256)
        w_raw = sb.tile([P, 2, PACK * C], F32, align_bytes=256)
        ad_raw = sb.tile([P, PACK * J], F32, align_bytes=256)
        bn_seed = sb.tile([P, N], F32, align_bytes=256)
        bn_sb = sb.tile([P, N], F32, align_bytes=256)
        ni_sb = sb.tile([P, PACK], F32, align_bytes=128)

        x_bf = sb.tile([P, PACK, G, R * PACK], BF16, align_bytes=128)
        w_bf = sb.tile([P, 2, C * PACK], BF16, align_bytes=128)
        ad_bf = sb.tile([P, J * PACK], BF16, align_bytes=128)
        h_bf = sb.tile([P, 4, C * PACK], BF16, align_bytes=128)
        h_rows = sb.tile([P, 2, C * PACK], BF16, align_bytes=128)

        x_codes = sb.tile([P, PACK, P], U32, align_bytes=128)
        x_scales = sb.tile([P, PACK, P], U8, align_bytes=128)
        w_codes = sb.tile([P, 2, C], U32, align_bytes=128)
        w_scales = sb.tile([P, 2, C], U8, align_bytes=128)
        ad_codes = sb.tile([P, J], U32, align_bytes=128)
        ad_scales = sb.tile([P, J], U8, align_bytes=128)
        h_codes = sb.tile([P, 4, C], U32, align_bytes=128)
        h_scales = sb.tile([P, 4, C], U8, align_bytes=128)

        biased = sb.tile([P, G, N], F32, align_bytes=256)
        result = sb.tile([P, G, N], F32, align_bytes=256)

        banks0 = [ps.tile([P, N], F32, name="tile0_%d" % k) for k in range(2)]
        banks2 = [ps.tile([P, N], F32, name="tile2_%d" % k) for k in range(PACK)]
        bank1 = ps.tile([P, N], F32)
        bank3 = ps.tile([P, N], F32)

        def z(c, t):
            if c % 2 == 0:
                return banks0[c // 2][:, t * C : (t + 1) * C]
            return banks2[t][:, (c // 2) * C : (c // 2 + 1) * C]

        def y(g, c0, c1):
            if g == 0:
                return banks0[c0 // 2][:, c0 * C : c1 * C]
            if g == 2:
                return banks2[c0 // 2][:, (2 + c0 % 2) * C : (2 + c0 % 2 + c1 - c0) * C]
            return (bank1 if g == 1 else bank3)[:, c0 * C : c1 * C]

        def load_w(queue, tile, s):
            r = FIRST_ROWS[tile]
            c = 2 * s + tile
            queue.dma_start(
                out=w_raw[r : r + R, s, :].rearrange("p (j n) -> p j n", j=PACK),
                in_=w[:, c * C : (c + 1) * C].rearrange("(p j) n -> p j n", j=PACK),
            )

        def load_x(queue, tile, g0, g1):
            r = FIRST_ROWS[tile]
            queue.dma_start(
                out=x_raw[r : r + R, g0:g1, :],
                in_=x[g0:g1].rearrange("g (p j) i -> p g (j i)", j=PACK),
            )

        def copy(engine, out_ap, in_ap):
            if engine == "vector":
                nc.vector.tensor_copy(out=out_ap, in_=in_ap)
            else:
                nc.scalar.copy(out=out_ap, in_=in_ap)

        def group_x(engine, g, t0, t1):
            copy(
                engine,
                x_bf[0:SPAN, t0:t1, g, :].rearrange("q t (p j) -> q p j t", j=PACK),
                x_raw[0:SPAN, g, :].rearrange("q (j p t) -> q p j t", j=PACK, t=PACK)[:, :, :, t0:t1],
            )

        def group_rows(engine, out_ap, in_ap):
            copy(
                engine,
                out_ap.rearrange("q (c i j) -> q c j i", i=4, j=PACK),
                in_ap.rearrange("q (j c i) -> q c j i", i=4, j=PACK),
            )

        def group_h(engine, c, n0, n1):
            copy(
                engine,
                h_bf[:, c, :].rearrange("q (c i t) -> q c t i", i=4, t=PACK)[:, n0 // 4 : n1 // 4],
                h_rows[:, c // 2, :].rearrange("q (t c i) -> q c t i", i=4, t=PACK)[:, n0 // 4 : n1 // 4],
            )

        def quantize(codes, scales, values):
            nc.vector.quantize_mx(out=codes.bitcast(FP8X4), scales=scales, in_=values)

        def project(tile, s, t):
            r = FIRST_ROWS[tile]
            nc.tensor.matmul_mx(
                out=z(2 * s + tile, t),
                lhsT=x_codes[r : r + R, t, :].bitcast(FP8X4),
                lhsT_scale=x_scales[r : r + R, t, :],
                rhs=w_codes[r : r + R, s, :].bitcast(FP8X4),
                rhs_scale=w_scales[r : r + R, s, :],
                start=True,
                stop=True,
            )

        def weigh_on_vector(c, n0, n1):
            nc.vector.tensor_tensor(
                out=h_bf[:, c, :].rearrange("q (n t) -> q n t", t=PACK)[:, n0:n1],
                in0=banks0[c // 2][:].rearrange("q (t n) -> q n t", t=PACK)[:, n0:n1],
                in1=ni_sb[:].unsqueeze(1).to_broadcast([P, n1 - n0, PACK]),
                op=ALU.mult,
            )

        def weigh_on_scalar(c, t):
            nc.scalar.activation(
                out=h_rows[:, c // 2, t * C : (t + 1) * C],
                in_=z(c, t),
                func=ACT.Copy,
                scale=ni_sb[:, t : t + 1],
            )

        def quantize_h(c):
            quantize(h_codes[:, c, :], h_scales[:, c, :], h_bf[:, c, :])

        def send(g, c):
            r = g * R
            nc.tensor.matmul_mx(
                out=y(g, c, c + 1),
                lhsT=ad_codes[r : r + R, :].bitcast(FP8X4),
                lhsT_scale=ad_scales[r : r + R, :],
                rhs=h_codes[r : r + R, c, :].bitcast(FP8X4),
                rhs_scale=h_scales[r : r + R, c, :],
                start=True,
                stop=True,
            )

        def finish(g, c0, c1):
            cols = slice(c0 * C, c1 * C)
            nc.vector.tensor_tensor(out=biased[:, g, cols], in0=y(g, c0, c1), in1=bn_sb[:, cols], op=ALU.add)
            nc.scalar.activation(out=result[:, g, cols], in_=biased[:, g, cols], func=ACT.Relu)
            nc.sync.dma_start(out=out[g, :, cols], in_=result[:, g, cols])

        for tile in range(2):
            load_w(queues[tile], tile, 0)
        for g0, g1 in ((0, 2), (2, 3), (3, 4)):
            for tile in range(2):
                load_x(queues[tile], tile, g0, g1)
        for tile in range(2):
            load_w(nc.sync, tile, 1)
        nc.sync.dma_start(out=ad_raw[:], in_=ad.rearrange("g (p t) j -> (g p) (t j)", t=PACK))
        nc.sync.dma_start(out=ni_sb[:], in_=ni.rearrange("g (p t) o -> (g p) (t o)", t=PACK))
        seeds = bn_seed[R : R + 4 * SEEDS : 4, :]
        nc.sync.dma_start(out=seeds, in_=bn[0].partition_broadcast(SEEDS))
        for c0, c1 in ((0, 2 * C), (2 * C, N)):
            nc.sync.dma_start(
                out=bn_sb[:, c0:c1],
                in_=seeds[:, c0:c1].unsqueeze(1).to_broadcast([SEEDS, P // SEEDS, c1 - c0]),
            )

        nc.vector.memset(w_raw[R : 2 * R, 0, 0:EARLY], 0.0)
        nc.scalar.activation(out=w_raw[R : 2 * R, 1, 0:EARLY], in_=w_raw[R : 2 * R, 0, 0:EARLY], func=ACT.Relu)
        nc.vector.memset(w_raw[R : 2 * R, 0, EARLY:], 0.0)
        for g in range(G):
            nc.vector.memset(x_raw[R : 2 * R, g, :], 0.0)
        nc.vector.memset(w_raw[R : 2 * R, 1, EARLY:], 0.0)

        group_rows("vector", w_bf[0:SPAN, 0, :], w_raw[0:SPAN, 0, :])
        group_x("vector", 0, 0, PACK)
        group_x("scalar", 1, 0, PACK)
        group_x("vector", 2, 0, PACK)
        group_x("vector", 3, 0, 2)
        group_x("scalar", 3, 2, PACK)
        quantize(w_codes[0:SPAN, 0, :], w_scales[0:SPAN, 0, :], w_bf[0:SPAN, 0, :])
        group_rows("scalar", w_bf[0:SPAN, 1, :], w_raw[0:SPAN, 1, :])
        for t in range(PACK):
            quantize(x_codes[0:SPAN, t, :], x_scales[0:SPAN, t, :], x_bf[0:SPAN, t].rearrange("q g k -> q (g k)"))
            for tile in range(2):
                project(tile, 0, t)
        group_rows("vector", ad_bf[:], ad_raw[:])
        quantize(w_codes[0:SPAN, 1, :], w_scales[0:SPAN, 1, :], w_bf[0:SPAN, 1, :])
        for t in range(PACK):
            weigh_on_scalar(1, t)
        for tile in range(2):
            for t in range(PACK):
                project(tile, 1, t)

        weigh_on_vector(0, 0, C)
        group_h("scalar", 1, SHARE, C)
        group_h("vector", 1, 0, SHARE)
        quantize(ad_codes[:], ad_scales[:], ad_bf[:])
        quantize_h(0)
        quantize_h(1)
        for t in range(PACK):
            weigh_on_scalar(3, t)
        for c in (0, 1):
            for g in (1, 3, 0):
                send(g, c)
        for c in (0, 1):
            send(2, c)
        group_h("scalar", 3, SHARE, C)
        weigh_on_vector(2, 0, C)
        group_h("vector", 3, 0, SHARE)
        finish(1, 0, 2)
        quantize_h(2)
        quantize_h(3)
        finish(3, 0, 2)
        finish(0, 0, 2)
        finish(2, 0, 2)
        for g in (1, 3, 0, 2):
            for c in (2, 3):
                send(g, c)
        for g in (1, 3, 0, 2):
            finish(g, 2, 4)
